import numpy as np, ml_dtypes
CORES = [3,7,11,15,131,135,139,143]
N = 8
F = 128
def setup_inputs(rng):
    return {"a": rng.standard_normal((N, 128, 128), dtype=np.float32).astype(ml_dtypes.bfloat16), "b": rng.standard_normal((N, 128, F), dtype=np.float32).astype(ml_dtypes.bfloat16)}
def setup_inputs_big(rng):
    d = setup_inputs(rng)
    for k in ("a", "b"): d[k] = (d[k].astype(np.float32) * 1024.0).astype(d[k].dtype)
    return d
def setup_inputs_small(rng):
    d = setup_inputs(rng)
    for k in ("a", "b"): d[k] = (d[k].astype(np.float32) * (1 / 1024.0)).astype(d[k].dtype)
    return d
def setup_inputs_apart(rng):
    d = setup_inputs(rng)
    f = (10.0 ** rng.permutation(np.linspace(-1.5, 1.5, N))).astype(np.float32).reshape(N, 1, 1)
    for k in ("a", "b"): d[k] = (d[k].astype(np.float32) * f).astype(d[k].dtype)
    return d
def reference(a, b):
    s = (a.astype(np.float64).sum(axis=0).T @ b.astype(np.float64).sum(axis=0)).astype(ml_dtypes.bfloat16 if a.dtype != np.float64 else np.float64)
    return {"y": np.broadcast_to(s, (N,) + s.shape)}

@@ -1,0 +1,111 @@
+from concourse.bass import DstId, RemoteDMATransfer
+
+K = 128
+W = 256
+
+SCRATCH = {
+    "own": ("dram", [K, W], "bfloat16"),
+    "land": ("dram", [3, K, W], "bfloat16"),
+    "near": ("sbuf", [K, W], "bfloat16"),
+    "far": ("sbuf", [K, W], "bfloat16"),
+    "acc": ("psum", [K, 128], "float32"),
+    "ysb": ("sbuf", [K, 128], "bfloat16"),
+}
+SEMAPHORES = ["loaded", "raw", "near_in", "far_in", "sent", "mm", "cast", "stored"]
+
+ONCHIP_OWN_ENGINES = False
+
+
+def _count(mask):
+    return bin(mask).count("1")
+
+
+def rank_program(g, core, T, topo):
+    if T.rank_of(core) is None:
+        return
+    S = T.sem
+    ranks = list(T.cores)
+
+    def host_group(c):
+        return [x for x in ranks if topo.host(x) == topo.host(c)]
+
+    def slot(src, dst):
+        return [x for x in host_group(dst) if x != dst].index(src)
+
+    def dst_id(d):
+        rid, pid = topo.addr(d, core)
+        return DstId(rid=rid, pnc=pid)
+
+    group = host_group(core)
+    neighbour = [x for x in group if x != core and topo.chip(x) == topo.chip(core)][0]
+    mates = [x for x in group if topo.mates(x, core)]
+    peer = [x for x in ranks if topo.same_plane(x, core) and topo.die(x) == topo.die(core)][0]
+    for d in mates + [neighbour, peer]:
+        assert topo.may_write(core, d)
+
+    off_mask = topo.mask(core, peer)
+    for d in mates:
+        off_mask &= topo.mask(core, d)
+    if ONCHIP_OWN_ENGINES:
+        on_mask = topo.mask(core, neighbour) & ~off_mask
+    else:
+        on_mask = 0
+    n_off, n_on = _count(off_mask), _count(on_mask)
+
+    g.sync.dma_start(T.own[:, 0:128], T.a[:, :]).then_inc(S.loaded, 16)
+    g.scalar.dma_start(T.own[:, 128:256], T.b[:, :]).then_inc(S.loaded, 16)
+    g.wait_ge(S.loaded, 32)
+
+    if on_mask:
+        round1 = [
+            RemoteDMATransfer(dst_ids=[dst_id(d) for d in mates], dma_engine_mask=off_mask, remote_sem=S.raw,
+                              srcs=[T.own[:, :]], dsts=[T.land[slot(core, d)] for d in mates]),
+            RemoteDMATransfer(dst_ids=[dst_id(neighbour)], dma_engine_mask=on_mask, remote_sem=S.raw,
+                              srcs=[T.own[:, :]], dsts=[T.land[slot(core, neighbour)]]),
+        ]
+        raw_total = 2 * n_off + n_on
+    else:
+        to = mates + [neighbour]
+        round1 = [
+            RemoteDMATransfer(dst_ids=[dst_id(d) for d in to], dma_engine_mask=off_mask, remote_sem=S.raw,
+                              srcs=[T.own[:, :]], dsts=[T.land[slot(core, d)] for d in to]),
+        ]
+        raw_total = 3 * n_off
+    g.remote_dma_fused(round1, local_sem=S.sent)
+    g.wait_ge(S.raw, raw_total)
+
+    pieces = [T.own[:, :]] + [T.land[k] for k in range(3)]
+    if on_mask:
+        round2 = [
+            RemoteDMATransfer(dst_ids=[dst_id(peer)], dma_engine_mask=off_mask, remote_sem=S.far_in,
+                              srcs=pieces, dsts=[T.far[:, :]], alu_op=1),
+            RemoteDMATransfer(dst_ids=[dst_id(neighbour)], dma_engine_mask=on_mask, remote_sem=S.near_in,
+                              srcs=pieces, dsts=[T.near[:, :]], alu_op=1),
+        ]
+        waits = [(S.near_in, n_on), (S.far_in, n_off)]
+    else:
+        round2 = [
+            RemoteDMATransfer(dst_ids=[dst_id(neighbour), dst_id(peer)], dma_engine_mask=off_mask, remote_sem=S.far_in,
+                              srcs=pieces, dsts=[T.near[:, :], T.far[:, :]], alu_op=1),
+        ]
+        waits = [(S.far_in, 2 * n_off), None]
+    g.remote_dma_fused(round2, local_sem=S.sent)
+
+    An, Bn = T.near[:, 0:128], T.near[:, 128:256]
+    Af, Bf = T.far[:, 0:128], T.far[:, 128:256]
+    g.tensor.wait_ge(waits[0][0], waits[0][1])
+    g.tensor.matmul(T.acc[:, :], An, Bn, True, False).then_inc(S.mm, 1)
+    if waits[1] is not None:
+        g.tensor.wait_ge(waits[1][0], waits[1][1])
+    g.tensor.matmul(T.acc[:, :], An, Bf, False, False).then_inc(S.mm, 1)
+    g.tensor.matmul(T.acc[:, :], Af, Bn, False, False).then_inc(S.mm, 1)
+    g.tensor.matmul(T.acc[:, :], Af, Bf, False, True).then_inc(S.mm, 1)
+
+    g.vector.wait_ge(S.mm, 4)
+    g.vector.tensor_copy(T.ysb[:, :], T.acc[:, :]).then_inc(S.cast, 1)
+
+    g.sync.wait_ge(S.cast, 1)
+    g.sync.dma_start(T.y[:, :], T.ysb[:, :]).then_inc(S.stored, 16)
+    g.sync.wait_ge(S.stored, 16)
+
+    g.wait_ge(S.sent, 2 * (n_off + n_on))

@@ -1,19 +1,21 @@
 from concourse.bass import DstId, RemoteDMATransfer
+from concourse.mybir import AluOpType
 
 K = 128
 W = 256
 
 SCRATCH = {
-    "own": ("dram", [K, W], "bfloat16"),
-    "land": ("dram", [3, K, W], "bfloat16"),
+    "own": ("sbuf", [K, W], "bfloat16"),
+    "land0": ("sbuf", [K, W], "bfloat16"),
+    "land1": ("sbuf", [K, W], "bfloat16"),
+    "land2": ("sbuf", [K, W], "bfloat16"),
     "near": ("sbuf", [K, W], "bfloat16"),
     "far": ("sbuf", [K, W], "bfloat16"),
-    "acc": ("psum", [K, 128], "float32"),
+    "part": ("psum", [K, 512], "float32"),
+    "acc": ("psum", [K, 512], "float32"),
     "ysb": ("sbuf", [K, 128], "bfloat16"),
 }
-SEMAPHORES = ["loaded", "raw", "near_in", "far_in", "sent", "mm", "cast", "stored"]
-
-ONCHIP_OWN_ENGINES = False
+SEMAPHORES = ["loaded", "raw0", "raw1", "raw2", "raw3", "vs", "near_ok", "far_in", "sent", "mm", "cast", "stored"]
 
 
 def _count(mask):
@@ -29,83 +31,67 @@ def rank_program(g, core, T, topo):
     def host_group(c):
         return [x for x in ranks if topo.host(x) == topo.host(c)]
 
-    def slot(src, dst):
-        return [x for x in host_group(dst) if x != dst].index(src)
+    def order(c):
+        grp = [x for x in host_group(c) if x != c]
+        m = [x for x in grp if topo.mates(x, c)]
+        return ([x for x in m if topo.die(x) == topo.die(c)] + [x for x in m if topo.die(x) != topo.die(c)]
+                + [x for x in grp if topo.chip(x) == topo.chip(c)])
+
+    def sem_of(src):
+        return S["raw%d" % host_group(src).index(src)]
 
     def dst_id(d):
         rid, pid = topo.addr(d, core)
         return DstId(rid=rid, pnc=pid)
 
-    group = host_group(core)
-    neighbour = [x for x in group if x != core and topo.chip(x) == topo.chip(core)][0]
-    mates = [x for x in group if topo.mates(x, core)]
+    to = order(core)
     peer = [x for x in ranks if topo.same_plane(x, core) and topo.die(x) == topo.die(core)][0]
-    for d in mates + [neighbour, peer]:
+    mask = topo.mask(core, peer)
+    for d in to + [peer]:
         assert topo.may_write(core, d)
-
-    off_mask = topo.mask(core, peer)
-    for d in mates:
-        off_mask &= topo.mask(core, d)
-    if ONCHIP_OWN_ENGINES:
-        on_mask = topo.mask(core, neighbour) & ~off_mask
-    else:
-        on_mask = 0
-    n_off, n_on = _count(off_mask), _count(on_mask)
+        mask &= topo.mask(core, d)
+    n = _count(mask)
 
     g.sync.dma_start(T.own[:, 0:128], T.a[:, :]).then_inc(S.loaded, 16)
     g.scalar.dma_start(T.own[:, 128:256], T.b[:, :]).then_inc(S.loaded, 16)
     g.wait_ge(S.loaded, 32)
 
-    if on_mask:
-        round1 = [
-            RemoteDMATransfer(dst_ids=[dst_id(d) for d in mates], dma_engine_mask=off_mask, remote_sem=S.raw,
-                              srcs=[T.own[:, :]], dsts=[T.land[slot(core, d)] for d in mates]),
-            RemoteDMATransfer(dst_ids=[dst_id(neighbour)], dma_engine_mask=on_mask, remote_sem=S.raw,
-                              srcs=[T.own[:, :]], dsts=[T.land[slot(core, neighbour)]]),
-        ]
-        raw_total = 2 * n_off + n_on
-    else:
-        to = mates + [neighbour]
-        round1 = [
-            RemoteDMATransfer(dst_ids=[dst_id(d) for d in to], dma_engine_mask=off_mask, remote_sem=S.raw,
-                              srcs=[T.own[:, :]], dsts=[T.land[slot(core, d)] for d in to]),
-        ]
-        raw_total = 3 * n_off
-    g.remote_dma_fused(round1, local_sem=S.sent)
-    g.wait_ge(S.raw, raw_total)
+    g.remote_dma_fused([
+        RemoteDMATransfer(dst_ids=[dst_id(d) for d in to], dma_engine_mask=mask, remote_sem=sem_of(core),
+                          srcs=[T.own[:, :]], dsts=[T["land%d" % order(d).index(core)][:, :] for d in to]),
+    ], local_sem=S.sent)
 
-    pieces = [T.own[:, :]] + [T.land[k] for k in range(3)]
-    if on_mask:
-        round2 = [
-            RemoteDMATransfer(dst_ids=[dst_id(peer)], dma_engine_mask=off_mask, remote_sem=S.far_in,
-                              srcs=pieces, dsts=[T.far[:, :]], alu_op=1),
-            RemoteDMATransfer(dst_ids=[dst_id(neighbour)], dma_engine_mask=on_mask, remote_sem=S.near_in,
-                              srcs=pieces, dsts=[T.near[:, :]], alu_op=1),
-        ]
-        waits = [(S.near_in, n_on), (S.far_in, n_off)]
-    else:
-        round2 = [
-            RemoteDMATransfer(dst_ids=[dst_id(neighbour), dst_id(peer)], dma_engine_mask=off_mask, remote_sem=S.far_in,
-                              srcs=pieces, dsts=[T.near[:, :], T.far[:, :]], alu_op=1),
-        ]
-        waits = [(S.far_in, 2 * n_off), None]
-    g.remote_dma_fused(round2, local_sem=S.sent)
+    part = T.part[:, 0:W]
+    g.vector.wait_ge(S.loaded, 32)
+    g.vector.tensor_copy(part, T.own[:, :]).then_inc(S.vs, 1)
+    for i, x in enumerate(to):
+        g.vector.wait_ge(sem_of(x), n)
+        g.vector.wait_ge(S.vs, i + 1)
+        piece = T["land%d" % i][:, :]
+        if i < len(to) - 1:
+            g.vector.tensor_tensor(part, part, piece, AluOpType.add).then_inc(S.vs, 1)
+        else:
+            g.vector.tensor_tensor(T.near[:, :], part, piece, AluOpType.add).then_inc(S.near_ok, 1)
+
+    rid, pid = topo.addr(peer, core)
+    g.wait_ge(S.near_ok, 1)
+    g.remote_dma(T.far[:, :], T.near[:, :], S.far_in, S.sent, pid, rid, mask)
 
     An, Bn = T.near[:, 0:128], T.near[:, 128:256]
     Af, Bf = T.far[:, 0:128], T.far[:, 128:256]
-    g.tensor.wait_ge(waits[0][0], waits[0][1])
-    g.tensor.matmul(T.acc[:, :], An, Bn, True, False).then_inc(S.mm, 1)
-    if waits[1] is not None:
-        g.tensor.wait_ge(waits[1][0], waits[1][1])
-    g.tensor.matmul(T.acc[:, :], An, Bf, False, False).then_inc(S.mm, 1)
-    g.tensor.matmul(T.acc[:, :], Af, Bn, False, False).then_inc(S.mm, 1)
-    g.tensor.matmul(T.acc[:, :], Af, Bf, False, True).then_inc(S.mm, 1)
+    acc = T.acc[:, 0:128]
+    g.tensor.wait_ge(S.near_ok, 1)
+    g.tensor.matmul(acc, An, Bn, True, False).then_inc(S.mm, 1)
+    g.tensor.wait_ge(S.far_in, n)
+    g.tensor.matmul(acc, An, Bf, False, False).then_inc(S.mm, 1)
+    g.tensor.matmul(acc, Af, Bn, False, False).then_inc(S.mm, 1)
+    g.tensor.matmul(acc, Af, Bf, False, True).then_inc(S.mm, 1)
 
     g.vector.wait_ge(S.mm, 4)
-    g.vector.tensor_copy(T.ysb[:, :], T.acc[:, :]).then_inc(S.cast, 1)
+    g.vector.tensor_copy(T.ysb[:, :], acc).then_inc(S.cast, 1)
 
     g.sync.wait_ge(S.cast, 1)
     g.sync.dma_start(T.y[:, :], T.ysb[:, :]).then_inc(S.stored, 16)
     g.sync.wait_ge(S.stored, 16)
 
-    g.wait_ge(S.sent, 2 * (n_off + n_on))
+    g.wait_ge(S.sent, 2 * n)

@@ -6,16 +6,22 @@ W = 256
 
 SCRATCH = {
     "own": ("sbuf", [K, W], "bfloat16"),
-    "land0": ("sbuf", [K, W], "bfloat16"),
-    "land1": ("sbuf", [K, W], "bfloat16"),
-    "land2": ("sbuf", [K, W], "bfloat16"),
+    "f1": ("sbuf", [K, W], "bfloat16"),
+    "nb": ("sbuf", [K, W], "bfloat16"),
+    "f2": ("sbuf", [K, W], "bfloat16"),
+    "pair": ("sbuf", [K, W], "bfloat16"),
+    "m1": ("sbuf", [K, W], "bfloat16"),
+    "m2": ("sbuf", [K, W], "bfloat16"),
     "near": ("sbuf", [K, W], "bfloat16"),
-    "far": ("sbuf", [K, W], "bfloat16"),
+    "ramp": ("sbuf", [K, K], "bfloat16"),
+    "ident": ("sbuf", [K, K], "bfloat16"),
     "part": ("psum", [K, 512], "float32"),
+    "q": ("psum", [K, 512], "float32"),
     "acc": ("psum", [K, 512], "float32"),
     "ysb": ("sbuf", [K, 128], "bfloat16"),
 }
-SEMAPHORES = ["loaded", "raw0", "raw1", "raw2", "raw3", "vs", "near_ok", "far_in", "sent", "mm", "cast", "stored"]
+SEMAPHORES = ["loaded", "ramp_ok", "id_ok", "r1", "sh0", "sh1", "x0", "x1", "vs", "pair_ok", "q_ok", "near_ok", "sent",
+              "mm", "cast", "stored"]
 
 
 def _count(mask):
@@ -27,65 +33,91 @@ def rank_program(g, core, T, topo):
         return
     S = T.sem
     ranks = list(T.cores)
+    hosts = sorted(set(topo.host(x) for x in ranks))
+    dies = sorted(set(topo.die(x) for x in ranks))
 
-    def host_group(c):
-        return [x for x in ranks if topo.host(x) == topo.host(c)]
+    def pick(cond):
+        found = [x for x in ranks if x != core and cond(x)]
+        assert len(found) == 1
+        return found[0]
 
-    def order(c):
-        grp = [x for x in host_group(c) if x != c]
-        m = [x for x in grp if topo.mates(x, c)]
-        return ([x for x in m if topo.die(x) == topo.die(c)] + [x for x in m if topo.die(x) != topo.die(c)]
-                + [x for x in grp if topo.chip(x) == topo.chip(c)])
+    same_die = lambda x: topo.die(x) == topo.die(core)
+    peer = pick(lambda x: topo.same_plane(x, core) and same_die(x))
+    peer_o = pick(lambda x: topo.same_plane(x, core) and not same_die(x))
+    nbr = pick(lambda x: topo.host(x) == topo.host(core) and topo.chip(x) == topo.chip(core))
+    mate = pick(lambda x: topo.mates(x, core) and same_die(x))
+    mate_o = pick(lambda x: topo.mates(x, core) and not same_die(x))
 
-    def sem_of(src):
-        return S["raw%d" % host_group(src).index(src)]
+    def sh_sem(src):
+        return S["sh%d" % hosts.index(topo.host(src))]
+
+    def x_sem(src):
+        return S["x%d" % dies.index(topo.die(src))]
 
     def dst_id(d):
         rid, pid = topo.addr(d, core)
         return DstId(rid=rid, pnc=pid)
 
-    to = order(core)
-    peer = [x for x in ranks if topo.same_plane(x, core) and topo.die(x) == topo.die(core)][0]
     mask = topo.mask(core, peer)
-    for d in to + [peer]:
+    for d in (peer, peer_o, nbr, mate, mate_o):
         assert topo.may_write(core, d)
         mask &= topo.mask(core, d)
     n = _count(mask)
 
     g.sync.dma_start(T.own[:, 0:128], T.a[:, :]).then_inc(S.loaded, 16)
     g.scalar.dma_start(T.own[:, 128:256], T.b[:, :]).then_inc(S.loaded, 16)
+    g.iota(T.ramp[:, :], [[-1, K]], 0, 1, allow_small_or_imprecise_dtypes=True).then_inc(S.ramp_ok, 1)
+    g.vector.wait_ge(S.ramp_ok, 1)
+    g.vector.tensor_scalar(T.ident[:, :], T.ramp[:, :], 0.0, None, AluOpType.is_equal).then_inc(S.id_ok, 1)
     g.wait_ge(S.loaded, 32)
 
+    rid, pid = topo.addr(peer, core)
+    g.remote_dma(T.f1[:, :], T.own[:, :], S.r1, S.sent, pid, rid, mask)
+
     g.remote_dma_fused([
-        RemoteDMATransfer(dst_ids=[dst_id(d) for d in to], dma_engine_mask=mask, remote_sem=sem_of(core),
-                          srcs=[T.own[:, :]], dsts=[T["land%d" % order(d).index(core)][:, :] for d in to]),
+        RemoteDMATransfer(dst_ids=[dst_id(nbr), dst_id(peer_o)], dma_engine_mask=mask, remote_sem=sh_sem(core),
+                          srcs=[T.own[:, :]], dsts=[T.nb[:, :], T.f2[:, :]]),
     ], local_sem=S.sent)
 
     part = T.part[:, 0:W]
+    add = AluOpType.add
     g.vector.wait_ge(S.loaded, 32)
     g.vector.tensor_copy(part, T.own[:, :]).then_inc(S.vs, 1)
-    for i, x in enumerate(to):
-        g.vector.wait_ge(sem_of(x), n)
-        g.vector.wait_ge(S.vs, i + 1)
-        piece = T["land%d" % i][:, :]
-        if i < len(to) - 1:
-            g.vector.tensor_tensor(part, part, piece, AluOpType.add).then_inc(S.vs, 1)
-        else:
-            g.vector.tensor_tensor(T.near[:, :], part, piece, AluOpType.add).then_inc(S.near_ok, 1)
+    g.vector.wait_ge(S.r1, n)
+    g.vector.wait_ge(S.vs, 1)
+    g.vector.tensor_tensor(T.pair[:, :], part, T.f1[:, :], add).then_inc(S.pair_ok, 1)
 
-    rid, pid = topo.addr(peer, core)
-    g.wait_ge(S.near_ok, 1)
-    g.remote_dma(T.far[:, :], T.near[:, :], S.far_in, S.sent, pid, rid, mask)
+    g.wait_ge(S.pair_ok, 1)
+    g.remote_dma_fused([
+        RemoteDMATransfer(dst_ids=[dst_id(mate), dst_id(mate_o)], dma_engine_mask=mask, remote_sem=x_sem(core),
+                          srcs=[T.pair[:, :]], dsts=[T.m1[:, :], T.m2[:, :]]),
+    ], local_sem=S.sent)
+
+    q = T.q[:, 0:W]
+    ident = T.ident[:, :]
+    g.tensor.wait_ge(S.id_ok, 1)
+    g.tensor.wait_ge(S.loaded, 32)
+    g.tensor.matmul(q, ident, T.own[:, :], True, False).then_inc(S.q_ok, 1)
+    g.tensor.wait_ge(S.r1, n)
+    g.tensor.matmul(q, ident, T.f1[:, :], False, False).then_inc(S.q_ok, 1)
+    g.tensor.wait_ge(sh_sem(nbr), n)
+    g.tensor.matmul(q, ident, T.nb[:, :], False, False).then_inc(S.q_ok, 1)
+    g.tensor.wait_ge(sh_sem(peer_o), n)
+    g.tensor.matmul(q, ident, T.f2[:, :], False, True).then_inc(S.q_ok, 1)
+
+    g.vector.wait_ge(S.q_ok, 4)
+    g.vector.wait_ge(x_sem(mate), n)
+    g.vector.tensor_tensor(T.near[:, :], q, T.m1[:, :], add).then_inc(S.near_ok, 1)
 
     An, Bn = T.near[:, 0:128], T.near[:, 128:256]
-    Af, Bf = T.far[:, 0:128], T.far[:, 128:256]
+    Am, Bm = T.m2[:, 0:128], T.m2[:, 128:256]
     acc = T.acc[:, 0:128]
     g.tensor.wait_ge(S.near_ok, 1)
     g.tensor.matmul(acc, An, Bn, True, False).then_inc(S.mm, 1)
-    g.tensor.wait_ge(S.far_in, n)
-    g.tensor.matmul(acc, An, Bf, False, False).then_inc(S.mm, 1)
-    g.tensor.matmul(acc, Af, Bn, False, False).then_inc(S.mm, 1)
-    g.tensor.matmul(acc, Af, Bf, False, True).then_inc(S.mm, 1)
+    g.tensor.wait_ge(x_sem(mate_o), n)
+    g.tensor.matmul(acc, An, Bm, False, False).then_inc(S.mm, 1)
+    g.tensor.matmul(acc, Am, Bn, False, False).then_inc(S.mm, 1)
+    g.tensor.matmul(acc, Am, Bm, False, True).then_inc(S.mm, 1)
 
     g.vector.wait_ge(S.mm, 4)
     g.vector.tensor_copy(T.ysb[:, :], acc).then_inc(S.cast, 1)
@@ -94,4 +126,4 @@ def rank_program(g, core, T, topo):
     g.sync.dma_start(T.y[:, :], T.ysb[:, :]).then_inc(S.stored, 16)
     g.sync.wait_ge(S.stored, 16)
 
-    g.wait_ge(S.sent, 2 * n)
+    g.wait_ge(S.sent, 3 * n)

from concourse.bass import DstId, RemoteDMATransfer
from concourse.mybir import AluOpType

K = 128
W = 256

SCRATCH = {
    "own": ("sbuf", [K, W], "bfloat16"),
    "f1": ("sbuf", [K, W], "bfloat16"),
    "nb": ("sbuf", [K, W], "bfloat16"),
    "f2": ("sbuf", [K, W], "bfloat16"),
    "pair": ("sbuf", [K, W], "bfloat16"),
    "m1": ("sbuf", [K, W], "bfloat16"),
    "m2": ("sbuf", [K, W], "bfloat16"),
    "near": ("sbuf", [K, W], "bfloat16"),
    "ramp": ("sbuf", [K, K], "bfloat16"),
    "ident": ("sbuf", [K, K], "bfloat16"),
    "part": ("psum", [K, 512], "float32"),
    "q": ("psum", [K, 512], "float32"),
    "acc": ("psum", [K, 512], "float32"),
    "ysb": ("sbuf", [K, 128], "bfloat16"),
}
SEMAPHORES = ["loaded", "ramp_ok", "id_ok", "r1", "sh0", "sh1", "x0", "x1", "vs", "pair_ok", "q_ok", "near_ok", "sent",
              "mm", "cast", "stored"]


def _count(mask):
    return bin(mask).count("1")


def rank_program(g, core, T, topo):
    if T.rank_of(core) is None:
        return
    S = T.sem
    ranks = list(T.cores)
    hosts = sorted(set(topo.host(x) for x in ranks))
    dies = sorted(set(topo.die(x) for x in ranks))

    def pick(cond):
        found = [x for x in ranks if x != core and cond(x)]
        assert len(found) == 1
        return found[0]

    same_die = lambda x: topo.die(x) == topo.die(core)
    peer = pick(lambda x: topo.same_plane(x, core) and same_die(x))
    peer_o = pick(lambda x: topo.same_plane(x, core) and not same_die(x))
    nbr = pick(lambda x: topo.host(x) == topo.host(core) and topo.chip(x) == topo.chip(core))
    mate = pick(lambda x: topo.mates(x, core) and same_die(x))
    mate_o = pick(lambda x: topo.mates(x, core) and not same_die(x))

    def sh_sem(src):
        return S["sh%d" % hosts.index(topo.host(src))]

    def x_sem(src):
        return S["x%d" % dies.index(topo.die(src))]

    def dst_id(d):
        rid, pid = topo.addr(d, core)
        return DstId(rid=rid, pnc=pid)

    mask = topo.mask(core, peer)
    for d in (peer, peer_o, nbr, mate, mate_o):
        assert topo.may_write(core, d)
        mask &= topo.mask(core, d)
    n = _count(mask)

    g.sync.dma_start(T.own[:, 0:128], T.a[:, :]).then_inc(S.loaded, 16)
    g.scalar.dma_start(T.own[:, 128:256], T.b[:, :]).then_inc(S.loaded, 16)
    g.iota(T.ramp[:, :], [[-1, K]], 0, 1, allow_small_or_imprecise_dtypes=True).then_inc(S.ramp_ok, 1)
    g.vector.wait_ge(S.ramp_ok, 1)
    g.vector.tensor_scalar(T.ident[:, :], T.ramp[:, :], 0.0, None, AluOpType.is_equal).then_inc(S.id_ok, 1)
    g.wait_ge(S.loaded, 32)

    rid, pid = topo.addr(peer, core)
    g.remote_dma(T.f1[:, :], T.own[:, :], S.r1, S.sent, pid, rid, mask)

    g.remote_dma_fused([
        RemoteDMATransfer(dst_ids=[dst_id(nbr), dst_id(peer_o)], dma_engine_mask=mask, remote_sem=sh_sem(core),
                          srcs=[T.own[:, :]], dsts=[T.nb[:, :], T.f2[:, :]]),
    ], local_sem=S.sent)

    part = T.part[:, 0:W]
    add = AluOpType.add
    g.vector.wait_ge(S.loaded, 32)
    g.vector.tensor_copy(part, T.own[:, :]).then_inc(S.vs, 1)
    g.vector.wait_ge(S.r1, n)
    g.vector.wait_ge(S.vs, 1)
    g.vector.tensor_tensor(T.pair[:, :], part, T.f1[:, :], add).then_inc(S.pair_ok, 1)

    g.wait_ge(S.pair_ok, 1)
    g.remote_dma_fused([
        RemoteDMATransfer(dst_ids=[dst_id(mate), dst_id(mate_o)], dma_engine_mask=mask, remote_sem=x_sem(core),
                          srcs=[T.pair[:, :]], dsts=[T.m1[:, :], T.m2[:, :]]),
    ], local_sem=S.sent)

    q = T.q[:, 0:W]
    ident = T.ident[:, :]
    g.tensor.wait_ge(S.id_ok, 1)
    g.tensor.wait_ge(S.loaded, 32)
    g.tensor.matmul(q, ident, T.own[:, :], True, False).then_inc(S.q_ok, 1)
    g.tensor.wait_ge(S.r1, n)
    g.tensor.matmul(q, ident, T.f1[:, :], False, False).then_inc(S.q_ok, 1)
    g.tensor.wait_ge(sh_sem(nbr), n)
    g.tensor.matmul(q, ident, T.nb[:, :], False, False).then_inc(S.q_ok, 1)
    g.tensor.wait_ge(sh_sem(peer_o), n)
    g.tensor.matmul(q, ident, T.f2[:, :], False, True).then_inc(S.q_ok, 1)

    g.vector.wait_ge(S.q_ok, 4)
    g.vector.wait_ge(x_sem(mate), n)
    g.vector.tensor_tensor(T.near[:, :], q, T.m1[:, :], add).then_inc(S.near_ok, 1)

    An, Bn = T.near[:, 0:128], T.near[:, 128:256]
    Am, Bm = T.m2[:, 0:128], T.m2[:, 128:256]
    acc = T.acc[:, 0:128]
    g.tensor.wait_ge(S.near_ok, 1)
    g.tensor.matmul(acc, An, Bn, True, False).then_inc(S.mm, 1)
    g.tensor.wait_ge(x_sem(mate_o), n)
    g.tensor.matmul(acc, An, Bm, False, False).then_inc(S.mm, 1)
    g.tensor.matmul(acc, Am, Bn, False, False).then_inc(S.mm, 1)
    g.tensor.matmul(acc, Am, Bm, False, True).then_inc(S.mm, 1)

    g.vector.wait_ge(S.mm, 4)
    g.vector.tensor_copy(T.ysb[:, :], acc).then_inc(S.cast, 1)

    g.sync.wait_ge(S.cast, 1)
    g.sync.dma_start(T.y[:, :], T.ysb[:, :]).then_inc(S.stored, 16)
    g.sync.wait_ge(S.stored, 16)

    g.wait_ge(S.sent, 3 * n)
